import numpy as np
import ml_dtypes


def mxq(x, axis, fmt="e4m3"):
    dtype, down = {"e4m3": (ml_dtypes.float8_e4m3fn, 7), "e5m2": (ml_dtypes.float8_e5m2, 14)}[fmt]
    v = np.moveaxis(np.asarray(x, np.float32).astype(ml_dtypes.bfloat16).astype(np.float64), axis, -1)
    blocks = v.reshape(v.shape[:-1] + (-1, 32))
    amax = np.abs(blocks).max(-1, keepdims=True)
    byte = np.maximum(np.where(amax > 0, np.frexp(amax)[1] - 1 + 127, 0) - down, 1)
    scale = np.exp2(byte - 127.0)
    codes = (blocks / scale).astype(np.float32).astype(dtype).astype(np.float64)
    return np.moveaxis((codes * scale).reshape(v.shape), -1, axis)


WIDE = False


def mx_kscale(k):
    if not WIDE:
        return np.ones(k)
    levels = np.array([10, -10, 5, -5, 0])
    if k % 512:
        return np.exp2(np.random.permutation(np.resize(levels, k // 32))).repeat(32)
    a = np.empty((k // 512, 16))
    for p in range(k // 512):
        a[p, :8] = np.random.permutation(np.resize(levels, 8))
        for g in range(8):
            far = levels[np.abs(levels - a[p, g]) >= 10]
            a[p, g + 8] = far[np.random.randint(len(far))]
    return np.exp2(a.ravel()).repeat(32)


def f64(x):
    return np.asarray(x).astype(np.float64)


def striped8(idx):
    return np.concatenate([x.reshape(-1, 16).T for x in idx]).astype(np.uint16)


def runs(offs, k):
    lists = np.stack([offs[16 * r : 16 * r + 16].T.reshape(-1) for r in range(8)]).astype(np.int64)
    return lists[np.arange(k) % 512 // 64]


def pack_weight(w):
    k, n = w.shape
    w = f64(np.asarray(w, np.float32).astype(ml_dtypes.bfloat16)).reshape(k // 32, 32, n)
    amax = np.abs(w).max(1)
    byte = np.clip(np.where(amax > 0, np.frexp(amax)[1] - 1 + 127 - 7, 1), 1, 254)
    scaled = (w * np.exp2(127.0 - byte)[:, None, :]).reshape(k, n).astype(np.float32)
    words = np.ascontiguousarray(scaled.reshape(k // 512, 128, 4, n).transpose(0, 1, 3, 2)).astype(ml_dtypes.float8_e4m3fn).view(np.uint8)
    return words, np.ascontiguousarray(byte.astype(np.uint8).reshape(k // 512, 16, n))


def unpack_weight(words, scales):
    g, p, n, _ = words.shape
    vals = np.ascontiguousarray(words).view(ml_dtypes.float8_e4m3fn).astype(np.float64) * np.repeat(np.exp2(scales.astype(np.float64) - 127.0), 8, axis=1)[..., None]
    return vals.transpose(0, 1, 3, 2).reshape(g * 512, n)


def relu(v):
    return np.maximum(v, 0.0)


K, T, S, N = 512, 2048, 512, 128


def setup_inputs():
    n = np.random.standard_normal
    s = mx_kscale(K)[:, None]
    packed_xT = pack_weight(n((K, T)) * s)
    return {
        "x_words": packed_xT[0],
        "x_scales": packed_xT[1],
        "w1": (n((K, N)) / np.sqrt(K) / s).astype(np.float32),
        "w2": (n((K, N)) / np.sqrt(K) / s).astype(np.float32),
        "offs": striped8(np.stack([np.random.permutation(T)[:S] for _ in range(8)])),
        "old": striped8(np.stack([np.random.permutation(T)[:S] for _ in range(8)])),
    }


def reference(x_words, x_scales, w1, w2, offs, old):
    xq = unpack_weight(x_words, x_scales)[np.arange(K)[:, None], runs(offs, K)]
    y = mxq(f64(w1), 0, "e4m3").T @ xq
    xold = unpack_weight(x_words, x_scales)[np.arange(K)[:, None], runs(old, K)]
    e = mxq(f64(w2), 0, "e4m3").T @ xold
    return relu(y - e)

@@ -1,0 +1,93 @@
+from contextlib import ExitStack
+
+import concourse.mybir as mybir
+
+K, T, S, M = 512, 2048, 512, 128
+FLOPS = 2 * 2 * K * M * S
+
+F32 = mybir.dt.float32
+BF16 = mybir.dt.bfloat16
+I32 = mybir.dt.int32
+U32 = mybir.dt.uint32
+U16 = mybir.dt.uint16
+U8 = mybir.dt.uint8
+FP8X4 = mybir.dt.float8_e4m3fn_x4
+ACT = mybir.ActivationFunctionType
+
+P = 128
+PACK = 4
+HALF = S // 2
+
+
+def tile_picked_phdiff_relu_p_kernel(tc, x_words, x_scales, w1, w2, offs, old, out):
+    nc = tc.nc
+    with ExitStack() as ctx:
+        keep = ctx.enter_context(tc.tile_pool(name="keep", bufs=1))
+        psum = ctx.enter_context(tc.psum_pool(name="psum", bufs=1))
+
+        scale_table = keep.tile([P, T], U8, name="scale_table", align_bytes=64)
+        nc.vector.memset(scale_table[:].bitcast(I32), 0)
+
+        lists = [keep.tile([P, S // 16], U16, name="list%d" % i) for i in range(2)]
+        nc.sync.dma_start(lists[0][:], offs)
+        nc.sync.dma_start(lists[1][:], old)
+        nc.sync.dma_start(scale_table[0:P:8, :].bitcast(I32), x_scales[0].bitcast(I32))
+
+        word_table = keep.tile([P, T], U32, name="word_table", align_bytes=64)
+        nc.sync.dma_start(word_table[:].bitcast(I32), x_words[0].rearrange("p n t -> p (n t)").bitcast(I32))
+        raw = [keep.tile([P, PACK, M], F32, name="raw%d" % i, tag="slot%d" % i, align_bytes=64) for i in range(2)]
+        for i, w in enumerate((w1, w2)):
+            nc.sync.dma_start(raw[i][:], w.rearrange("(p j) m -> p j m", j=PACK))
+
+        planes = [keep.tile([P, S], U8, name="plane%d" % i, align_bytes=64) for i in range(2)]
+        for plane in planes:
+            nc.vector.memset(plane[:].bitcast(I32), 0)
+
+        for i in range(2):
+            picked = keep.tile([P, S], U8, name="picked%d" % i, align_bytes=64)
+            nc.vector.tensor_copy(picked[:], scale_table[:].indirect(lists[i][:]))
+            for s in range(4):
+                nc.sync.dma_start(planes[i][s:P:32, :].bitcast(I32), picked[8 * s : P : 32, :].bitcast(I32))
+
+        def quantize(i, sign):
+            grouped = keep.tile([P, M, PACK], BF16, name="grouped%d" % i, align_bytes=64)
+            nc.scalar.activation(grouped[:], raw[i][:].rearrange("p j m -> p m j"), ACT.Copy, scale=sign)
+            w_codes = keep.tile([P, M], U32, name="w_codes%d" % i, align_bytes=64)
+            w_scales = keep.tile([P, M], U8, name="w_scales%d" % i, align_bytes=64)
+            nc.vector.quantize_mx(out=w_codes[:].bitcast(FP8X4), scales=w_scales[:], in_=grouped[:].rearrange("p m j -> p (m j)"))
+            return w_codes, w_scales
+
+        acc = [psum.tile([M, HALF], F32, name="acc%d" % h) for h in range(2)]
+
+        def product(i, h, weights, moving):
+            nc.tensor.matmul_mx(
+                out=acc[h][:],
+                lhsT=weights[0][:].bitcast(FP8X4),
+                lhsT_scale=weights[1][:],
+                rhs=moving.bitcast(FP8X4),
+                rhs_scale=planes[i][:, h * HALF : (h + 1) * HALF],
+                start=(i == 0),
+                stop=(i == 1),
+            )
+
+        def gather_old(h):
+            before = keep.tile([P, HALF], U32, name="before%d" % h, tag="slot%d" % h, align_bytes=64)
+            nc.vector.tensor_copy(before[:], word_table[:].indirect(lists[1][:, h * HALF // 16 : (h + 1) * HALF // 16]))
+            return before
+
+        def finish(h, weights, before):
+            product(1, h, weights, before[:])
+            result = keep.tile([M, HALF], F32, name="result%d" % h)
+            nc.scalar.activation(result[:], acc[h][:], ACT.Relu)
+            nc.scalar.dma_start(out[:, h * HALF : (h + 1) * HALF], result[:])
+
+        now = keep.tile([P, S], U32, name="now", align_bytes=64)
+        nc.vector.tensor_copy(now[:], word_table[:].indirect(lists[0][:]))
+        q1 = quantize(0, 1.0)
+        for h in range(2):
+            product(0, h, q1, now[:, h * HALF : (h + 1) * HALF])
+        first = gather_old(0)
+        q2 = quantize(1, -1.0)
+        second = gather_old(1)
+        finish(0, q2, first)
+        finish(1, q2, second)

@@ -17,6 +17,8 @@ ACT = mybir.ActivationFunctionType
 P = 128
 PACK = 4
 HALF = S // 2
+QUARTER = S // 4
+STRETCHES = ((0, HALF), (HALF, HALF + QUARTER), (HALF + QUARTER, S))
 
 
 def tile_picked_phdiff_relu_p_kernel(tc, x_words, x_scales, w1, w2, offs, old, out):
@@ -36,8 +38,8 @@ def tile_picked_phdiff_relu_p_kernel(tc, x_words, x_scales, w1, w2, offs, old, o
         word_table = keep.tile([P, T], U32, name="word_table", align_bytes=64)
         nc.sync.dma_start(word_table[:].bitcast(I32), x_words[0].rearrange("p n t -> p (n t)").bitcast(I32))
         raw = [keep.tile([P, PACK, M], F32, name="raw%d" % i, tag="slot%d" % i, align_bytes=64) for i in range(2)]
-        for i, w in enumerate((w1, w2)):
-            nc.sync.dma_start(raw[i][:], w.rearrange("(p j) m -> p j m", j=PACK))
+        nc.scalar.dma_start(raw[0][:], w1.rearrange("(p j) m -> p j m", j=PACK))
+        nc.sync.dma_start(raw[1][:], w2.rearrange("(p j) m -> p j m", j=PACK))
 
         planes = [keep.tile([P, S], U8, name="plane%d" % i, align_bytes=64) for i in range(2)]
         for plane in planes:
@@ -47,7 +49,8 @@ def tile_picked_phdiff_relu_p_kernel(tc, x_words, x_scales, w1, w2, offs, old, o
             picked = keep.tile([P, S], U8, name="picked%d" % i, align_bytes=64)
             nc.vector.tensor_copy(picked[:], scale_table[:].indirect(lists[i][:]))
             for s in range(4):
-                nc.sync.dma_start(planes[i][s:P:32, :].bitcast(I32), picked[8 * s : P : 32, :].bitcast(I32))
+                queue = nc.scalar if s % 2 else nc.sync
+                queue.dma_start(planes[i][s:P:32, :].bitcast(I32), picked[8 * s : P : 32, :].bitcast(I32))
 
         def quantize(i, sign):
             grouped = keep.tile([P, M, PACK], BF16, name="grouped%d" % i, align_bytes=64)
@@ -57,37 +60,38 @@ def tile_picked_phdiff_relu_p_kernel(tc, x_words, x_scales, w1, w2, offs, old, o
             nc.vector.quantize_mx(out=w_codes[:].bitcast(FP8X4), scales=w_scales[:], in_=grouped[:].rearrange("p m j -> p (m j)"))
             return w_codes, w_scales
 
-        acc = [psum.tile([M, HALF], F32, name="acc%d" % h) for h in range(2)]
+        acc = [psum.tile([M, b - a], F32, name="acc%d" % a) for a, b in STRETCHES]
 
-        def product(i, h, weights, moving):
+        def product(i, c, weights, moving):
+            a, b = STRETCHES[c]
             nc.tensor.matmul_mx(
-                out=acc[h][:],
+                out=acc[c][:],
                 lhsT=weights[0][:].bitcast(FP8X4),
                 lhsT_scale=weights[1][:],
                 rhs=moving.bitcast(FP8X4),
-                rhs_scale=planes[i][:, h * HALF : (h + 1) * HALF],
+                rhs_scale=planes[i][:, a:b],
                 start=(i == 0),
                 stop=(i == 1),
             )
 
-        def gather_old(h):
-            before = keep.tile([P, HALF], U32, name="before%d" % h, tag="slot%d" % h, align_bytes=64)
-            nc.vector.tensor_copy(before[:], word_table[:].indirect(lists[1][:, h * HALF // 16 : (h + 1) * HALF // 16]))
-            return before
-
-        def finish(h, weights, before):
-            product(1, h, weights, before[:])
-            result = keep.tile([M, HALF], F32, name="result%d" % h)
-            nc.scalar.activation(result[:], acc[h][:], ACT.Relu)
-            nc.scalar.dma_start(out[:, h * HALF : (h + 1) * HALF], result[:])
-
+        q1 = quantize(0, 1.0)
         now = keep.tile([P, S], U32, name="now", align_bytes=64)
         nc.vector.tensor_copy(now[:], word_table[:].indirect(lists[0][:]))
-        q1 = quantize(0, 1.0)
-        for h in range(2):
-            product(0, h, q1, now[:, h * HALF : (h + 1) * HALF])
-        first = gather_old(0)
+        for c, (a, b) in enumerate(STRETCHES):
+            product(0, c, q1, now[:, a:b])
+        first = keep.tile([P, HALF], U32, name="first", align_bytes=64)
+        nc.vector.tensor_copy(first[:], word_table[:].indirect(lists[1][:, : HALF // 16]))
         q2 = quantize(1, -1.0)
-        second = gather_old(1)
-        finish(0, q2, first)
-        finish(1, q2, second)
+        second = keep.tile([P, HALF], U32, name="second", tag="slot1", align_bytes=64)
+        nc.vector.tensor_copy(second[:], word_table[:].indirect(lists[1][:, HALF // 16 :]))
+
+        result = [keep.tile([M, b - a], F32, name="result%d" % a) for a, b in STRETCHES]
+        product(1, 0, q2, first[:])
+        nc.scalar.activation(result[0][:], acc[0][:], ACT.Relu)
+        nc.sync.dma_start(out[:, :HALF], result[0][:])
+        product(1, 1, q2, second[:, :QUARTER])
+        product(1, 2, q2, second[:, QUARTER:])
+        nc.scalar.activation(result[1][:], acc[1][:], ACT.Relu)
+        nc.sync.dma_start(out[:, HALF : HALF + QUARTER], result[1][:])
+        nc.scalar.activation(result[2][:], acc[2][:], ACT.Relu)
+        nc.scalar.dma_start(out[:, HALF + QUARTER :], result[2][:])

@@ -18,7 +18,7 @@ P = 128
 PACK = 4
 HALF = S // 2
 QUARTER = S // 4
-STRETCHES = ((0, HALF), (HALF, HALF + QUARTER), (HALF + QUARTER, S))
+STRETCHES = tuple((a, a + QUARTER) for a in range(0, S, QUARTER))
 
 
 def tile_picked_phdiff_relu_p_kernel(tc, x_words, x_scales, w1, w2, offs, old, out):
@@ -85,13 +85,14 @@ def tile_picked_phdiff_relu_p_kernel(tc, x_words, x_scales, w1, w2, offs, old, o
         second = keep.tile([P, HALF], U32, name="second", tag="slot1", align_bytes=64)
         nc.vector.tensor_copy(second[:], word_table[:].indirect(lists[1][:, HALF // 16 :]))
 
-        result = [keep.tile([M, b - a], F32, name="result%d" % a) for a, b in STRETCHES]
-        product(1, 0, q2, first[:])
-        nc.scalar.activation(result[0][:], acc[0][:], ACT.Relu)
-        nc.sync.dma_start(out[:, :HALF], result[0][:])
-        product(1, 1, q2, second[:, :QUARTER])
-        product(1, 2, q2, second[:, QUARTER:])
-        nc.scalar.activation(result[1][:], acc[1][:], ACT.Relu)
-        nc.sync.dma_start(out[:, HALF : HALF + QUARTER], result[1][:])
-        nc.scalar.activation(result[2][:], acc[2][:], ACT.Relu)
-        nc.scalar.dma_start(out[:, HALF + QUARTER :], result[2][:])
+        early = keep.tile([M, HALF], F32, name="early")
+        late = [keep.tile([M, QUARTER], F32, name="late%d" % c) for c in range(2)]
+        for c in range(2):
+            product(1, c, q2, first[:, c * QUARTER : (c + 1) * QUARTER])
+            nc.scalar.activation(early[:, c * QUARTER : (c + 1) * QUARTER], acc[c][:], ACT.Relu)
+        nc.sync.dma_start(out[:, :HALF], early[:])
+        for c, queue in enumerate((nc.sync, nc.scalar)):
+            a, b = STRETCHES[2 + c]
+            product(1, 2 + c, q2, second[:, c * QUARTER : (c + 1) * QUARTER])
+            nc.scalar.activation(late[c][:], acc[2 + c][:], ACT.Relu)
+            queue.dma_start(out[:, a:b], late[c][:])

@@ -49,12 +49,17 @@ def tile_picked_phdiff_relu_p_kernel(tc, x_words, x_scales, w1, w2, offs, old, o
             picked = keep.tile([P, S], U8, name="picked%d" % i, align_bytes=64)
             nc.vector.tensor_copy(picked[:], scale_table[:].indirect(lists[i][:]))
             for s in range(4):
-                queue = nc.scalar if s % 2 else nc.sync
+                queue = nc.sync if s % 2 else nc.scalar
                 queue.dma_start(planes[i][s:P:32, :].bitcast(I32), picked[8 * s : P : 32, :].bitcast(I32))
 
         def quantize(i, sign):
             grouped = keep.tile([P, M, PACK], BF16, name="grouped%d" % i, align_bytes=64)
-            nc.scalar.activation(grouped[:], raw[i][:].rearrange("p j m -> p m j"), ACT.Copy, scale=sign)
+            nc.scalar.activation(
+                grouped[:].rearrange("p (c i) j -> p c j i", i=PACK),
+                raw[i][:].rearrange("p j (c i) -> p c j i", i=PACK),
+                ACT.Copy,
+                scale=sign,
+            )
             w_codes = keep.tile([P, M], U32, name="w_codes%d" % i, align_bytes=64)
             w_scales = keep.tile([P, M], U8, name="w_scales%d" % i, align_bytes=64)
             nc.vector.quantize_mx(out=w_codes[:].bitcast(FP8X4), scales=w_scales[:], in_=grouped[:].rearrange("p m j -> p (m j)"))

@@ -49,7 +49,7 @@ def tile_picked_phdiff_relu_p_kernel(tc, x_words, x_scales, w1, w2, offs, old, o
             picked = keep.tile([P, S], U8, name="picked%d" % i, align_bytes=64)
             nc.vector.tensor_copy(picked[:], scale_table[:].indirect(lists[i][:]))
             for s in range(4):
-                queue = nc.sync if s % 2 else nc.scalar
+                queue = nc.sync if i else nc.scalar
                 queue.dma_start(planes[i][s:P:32, :].bitcast(I32), picked[8 * s : P : 32, :].bitcast(I32))
 
         def quantize(i, sign):

@@ -19,6 +19,7 @@ PACK = 4
 HALF = S // 2
 QUARTER = S // 4
 STRETCHES = tuple((a, a + QUARTER) for a in range(0, S, QUARTER))
+EARLY = 256
 
 
 def tile_picked_phdiff_relu_p_kernel(tc, x_words, x_scales, w1, w2, offs, old, out):
@@ -33,13 +34,16 @@ def tile_picked_phdiff_relu_p_kernel(tc, x_words, x_scales, w1, w2, offs, old, o
         lists = [keep.tile([P, S // 16], U16, name="list%d" % i) for i in range(2)]
         nc.sync.dma_start(lists[0][:], offs)
         nc.sync.dma_start(lists[1][:], old)
-        nc.sync.dma_start(scale_table[0:P:8, :].bitcast(I32), x_scales[0].bitcast(I32))
 
         word_table = keep.tile([P, T], U32, name="word_table", align_bytes=64)
-        nc.sync.dma_start(word_table[:].bitcast(I32), x_words[0].rearrange("p n t -> p (n t)").bitcast(I32))
+        words = x_words[0].rearrange("p n t -> p (n t)").bitcast(I32)
+        for a in range(0, EARLY, EARLY // 2):
+            nc.scalar.dma_start(word_table[:, a : a + EARLY // 2].bitcast(I32), words[:, a : a + EARLY // 2])
+        nc.scalar.dma_start(scale_table[0:P:8, :].bitcast(I32), x_scales[0].bitcast(I32))
+        nc.scalar.dma_start(word_table[:, EARLY:].bitcast(I32), words[:, EARLY:])
         raw = [keep.tile([P, PACK, M], F32, name="raw%d" % i, tag="slot%d" % i, align_bytes=64) for i in range(2)]
         nc.scalar.dma_start(raw[0][:], w1.rearrange("(p j) m -> p j m", j=PACK))
-        nc.sync.dma_start(raw[1][:], w2.rearrange("(p j) m -> p j m", j=PACK))
+        nc.scalar.dma_start(raw[1][:], w2.rearrange("(p j) m -> p j m", j=PACK))
 
         planes = [keep.tile([P, S], U8, name="plane%d" % i, align_bytes=64) for i in range(2)]
         for plane in planes:
@@ -49,8 +53,7 @@ def tile_picked_phdiff_relu_p_kernel(tc, x_words, x_scales, w1, w2, offs, old, o
             picked = keep.tile([P, S], U8, name="picked%d" % i, align_bytes=64)
             nc.vector.tensor_copy(picked[:], scale_table[:].indirect(lists[i][:]))
             for s in range(4):
-                queue = nc.sync if i else nc.scalar
-                queue.dma_start(planes[i][s:P:32, :].bitcast(I32), picked[8 * s : P : 32, :].bitcast(I32))
+                nc.sync.dma_start(planes[i][s:P:32, :].bitcast(I32), picked[8 * s : P : 32, :].bitcast(I32))
 
         def quantize(i, sign):
             grouped = keep.tile([P, M, PACK], BF16, name="grouped%d" % i, align_bytes=64)
@@ -79,12 +82,12 @@ def tile_picked_phdiff_relu_p_kernel(tc, x_words, x_scales, w1, w2, offs, old, o
                 stop=(i == 1),
             )
 
-        q1 = quantize(0, 1.0)
         now = keep.tile([P, S], U32, name="now", align_bytes=64)
         nc.vector.tensor_copy(now[:], word_table[:].indirect(lists[0][:]))
+        q1 = quantize(0, 1.0)
         for c, (a, b) in enumerate(STRETCHES):
             product(0, c, q1, now[:, a:b])
-        first = keep.tile([P, HALF], U32, name="first", align_bytes=64)
+        first = keep.tile([P, HALF], U32, name="first", tag="slot0", align_bytes=64)
         nc.vector.tensor_copy(first[:], word_table[:].indirect(lists[1][:, : HALF // 16]))
         q2 = quantize(1, -1.0)
         second = keep.tile([P, HALF], U32, name="second", tag="slot1", align_bytes=64)

@@ -19,7 +19,7 @@ PACK = 4
 HALF = S // 2
 QUARTER = S // 4
 STRETCHES = tuple((a, a + QUARTER) for a in range(0, S, QUARTER))
-EARLY = 256
+EARLY = 128
 
 
 def tile_picked_phdiff_relu_p_kernel(tc, x_words, x_scales, w1, w2, offs, old, out):
@@ -37,8 +37,8 @@ def tile_picked_phdiff_relu_p_kernel(tc, x_words, x_scales, w1, w2, offs, old, o
 
         word_table = keep.tile([P, T], U32, name="word_table", align_bytes=64)
         words = x_words[0].rearrange("p n t -> p (n t)").bitcast(I32)
-        for a in range(0, EARLY, EARLY // 2):
-            nc.scalar.dma_start(word_table[:, a : a + EARLY // 2].bitcast(I32), words[:, a : a + EARLY // 2])
+        for first_row in range(2):
+            nc.scalar.dma_start(word_table[first_row:P:2, :EARLY].bitcast(I32), words[first_row:P:2, :EARLY])
         nc.scalar.dma_start(scale_table[0:P:8, :].bitcast(I32), x_scales[0].bitcast(I32))
         nc.scalar.dma_start(word_table[:, EARLY:].bitcast(I32), words[:, EARLY:])
         raw = [keep.tile([P, PACK, M], F32, name="raw%d" % i, tag="slot%d" % i, align_bytes=64) for i in range(2)]

@@ -45,15 +45,23 @@ def tile_picked_phdiff_relu_p_kernel(tc, x_words, x_scales, w1, w2, offs, old, o
         nc.scalar.dma_start(raw[0][:], w1.rearrange("(p j) m -> p j m", j=PACK))
         nc.scalar.dma_start(raw[1][:], w2.rearrange("(p j) m -> p j m", j=PACK))
 
-        planes = [keep.tile([P, S], U8, name="plane%d" % i, align_bytes=64) for i in range(2)]
+        batches = (((0, 0, HALF), (1, 0, HALF)), ((0, HALF, S), (1, HALF, S)))
+        widths = [sum(b - a for i, a, b in batch) for batch in batches]
+        planes = [keep.tile([P, w], U8, name="plane%d" % n, align_bytes=64) for n, w in enumerate(widths)]
         for plane in planes:
             nc.vector.memset(plane[:].bitcast(I32), 0)
 
-        for i in range(2):
-            picked = keep.tile([P, S], U8, name="picked%d" % i, align_bytes=64)
-            nc.vector.tensor_copy(picked[:], scale_table[:].indirect(lists[i][:]))
+        where = {}
+        for n, batch in enumerate(batches):
+            picked = keep.tile([P, widths[n]], U8, name="picked%d" % n, align_bytes=64)
+            at = 0
+            for i, a, b in batch:
+                nc.vector.tensor_copy(picked[:, at : at + b - a], scale_table[:].indirect(lists[i][:, a // 16 : b // 16]))
+                for column in range(a, b, QUARTER):
+                    where[i, column] = planes[n][:, at + column - a : at + column - a + QUARTER]
+                at = at + b - a
             for s in range(4):
-                nc.sync.dma_start(planes[i][s:P:32, :].bitcast(I32), picked[8 * s : P : 32, :].bitcast(I32))
+                nc.sync.dma_start(planes[n][s:P:32, :].bitcast(I32), picked[8 * s : P : 32, :].bitcast(I32))
 
         def quantize(i, sign):
             grouped = keep.tile([P, M, PACK], BF16, name="grouped%d" % i, align_bytes=64)
@@ -77,7 +85,7 @@ def tile_picked_phdiff_relu_p_kernel(tc, x_words, x_scales, w1, w2, offs, old, o
                 lhsT=weights[0][:].bitcast(FP8X4),
                 lhsT_scale=weights[1][:],
                 rhs=moving.bitcast(FP8X4),
-                rhs_scale=planes[i][:, a:b],
+                rhs_scale=where[i, a],
                 start=(i == 0),
                 stop=(i == 1),
             )
@@ -85,8 +93,8 @@ def tile_picked_phdiff_relu_p_kernel(tc, x_words, x_scales, w1, w2, offs, old, o
         now = keep.tile([P, S], U32, name="now", align_bytes=64)
         nc.vector.tensor_copy(now[:], word_table[:].indirect(lists[0][:]))
         q1 = quantize(0, 1.0)
-        for c, (a, b) in enumerate(STRETCHES):
-            product(0, c, q1, now[:, a:b])
+        for c in range(2):
+            product(0, c, q1, now[:, c * QUARTER : (c + 1) * QUARTER])
         first = keep.tile([P, HALF], U32, name="first", tag="slot0", align_bytes=64)
         nc.vector.tensor_copy(first[:], word_table[:].indirect(lists[1][:, : HALF // 16]))
         q2 = quantize(1, -1.0)
@@ -99,6 +107,8 @@ def tile_picked_phdiff_relu_p_kernel(tc, x_words, x_scales, w1, w2, offs, old, o
             product(1, c, q2, first[:, c * QUARTER : (c + 1) * QUARTER])
             nc.scalar.activation(early[:, c * QUARTER : (c + 1) * QUARTER], acc[c][:], ACT.Relu)
         nc.sync.dma_start(out[:, :HALF], early[:])
+        for c in range(2, 4):
+            product(0, c, q1, now[:, c * QUARTER : (c + 1) * QUARTER])
         for c, queue in enumerate((nc.sync, nc.scalar)):
             a, b = STRETCHES[2 + c]
             product(1, 2 + c, q2, second[:, c * QUARTER : (c + 1) * QUARTER])

@@ -92,17 +92,17 @@ def tile_picked_phdiff_relu_p_kernel(tc, x_words, x_scales, w1, w2, offs, old, o
 
         now = keep.tile([P, S], U32, name="now", align_bytes=64)
         nc.vector.tensor_copy(now[:], word_table[:].indirect(lists[0][:]))
-        q1 = quantize(0, 1.0)
-        for c in range(2):
-            product(0, c, q1, now[:, c * QUARTER : (c + 1) * QUARTER])
-        first = keep.tile([P, HALF], U32, name="first", tag="slot0", align_bytes=64)
+        first = keep.tile([P, HALF], U32, name="first", align_bytes=64)
         nc.vector.tensor_copy(first[:], word_table[:].indirect(lists[1][:, : HALF // 16]))
+        q1 = quantize(0, 1.0)
         q2 = quantize(1, -1.0)
         second = keep.tile([P, HALF], U32, name="second", tag="slot1", align_bytes=64)
         nc.vector.tensor_copy(second[:], word_table[:].indirect(lists[1][:, HALF // 16 :]))
 
         early = keep.tile([M, HALF], F32, name="early")
         late = [keep.tile([M, QUARTER], F32, name="late%d" % c) for c in range(2)]
+        for c in range(2):
+            product(0, c, q1, now[:, c * QUARTER : (c + 1) * QUARTER])
         for c in range(2):
             product(1, c, q2, first[:, c * QUARTER : (c + 1) * QUARTER])
             nc.scalar.activation(early[:, c * QUARTER : (c + 1) * QUARTER], acc[c][:], ACT.Relu)

@@ -45,7 +45,7 @@ def tile_picked_phdiff_relu_p_kernel(tc, x_words, x_scales, w1, w2, offs, old, o
         nc.scalar.dma_start(raw[0][:], w1.rearrange("(p j) m -> p j m", j=PACK))
         nc.scalar.dma_start(raw[1][:], w2.rearrange("(p j) m -> p j m", j=PACK))
 
-        batches = (((0, 0, HALF), (1, 0, HALF)), ((0, HALF, S), (1, HALF, S)))
+        batches = (((0, 0, S), (1, 0, S)),)
         widths = [sum(b - a for i, a, b in batch) for batch in batches]
         planes = [keep.tile([P, w], U8, name="plane%d" % n, align_bytes=64) for n, w in enumerate(widths)]
         for plane in planes:

@@ -51,6 +51,11 @@ def tile_picked_phdiff_relu_p_kernel(tc, x_words, x_scales, w1, w2, offs, old, o
         for plane in planes:
             nc.vector.memset(plane[:].bitcast(I32), 0)
 
+        one = keep.tile([P, 1], F32, name="one")
+        nc.vector.memset(one[:], 1.0)
+        minus = keep.tile([P, 1], F32, name="minus")
+        nc.scalar.activation(minus[:], one[:], ACT.Copy, scale=-1.0)
+
         where = {}
         for n, batch in enumerate(batches):
             picked = keep.tile([P, widths[n]], U8, name="picked%d" % n, align_bytes=64)
@@ -61,7 +66,7 @@ def tile_picked_phdiff_relu_p_kernel(tc, x_words, x_scales, w1, w2, offs, old, o
                     where[i, column] = planes[n][:, at + column - a : at + column - a + QUARTER]
                 at = at + b - a
             for s in range(4):
-                nc.sync.dma_start(planes[n][s:P:32, :].bitcast(I32), picked[8 * s : P : 32, :].bitcast(I32))
+                (nc.sync, nc.scalar)[s % 2].dma_start(planes[n][s:P:32, :].bitcast(I32), picked[8 * s : P : 32, :].bitcast(I32))
 
         def quantize(i, sign):
             grouped = keep.tile([P, M, PACK], BF16, name="grouped%d" % i, align_bytes=64)
@@ -95,7 +100,7 @@ def tile_picked_phdiff_relu_p_kernel(tc, x_words, x_scales, w1, w2, offs, old, o
         first = keep.tile([P, HALF], U32, name="first", align_bytes=64)
         nc.vector.tensor_copy(first[:], word_table[:].indirect(lists[1][:, : HALF // 16]))
         q1 = quantize(0, 1.0)
-        q2 = quantize(1, -1.0)
+        q2 = quantize(1, minus[:])
         second = keep.tile([P, HALF], U32, name="second", tag="slot1", align_bytes=64)
         nc.vector.tensor_copy(second[:], word_table[:].indirect(lists[1][:, HALF // 16 :]))
 

@@ -18,7 +18,7 @@ P = 128
 PACK = 4
 HALF = S // 2
 QUARTER = S // 4
-STRETCHES = tuple((a, a + QUARTER) for a in range(0, S, QUARTER))
+STRETCHES = ((0, HALF), (HALF, HALF + QUARTER), (HALF + QUARTER, S))
 EARLY = 128
 
 
@@ -62,8 +62,9 @@ def tile_picked_phdiff_relu_p_kernel(tc, x_words, x_scales, w1, w2, offs, old, o
             at = 0
             for i, a, b in batch:
                 nc.vector.tensor_copy(picked[:, at : at + b - a], scale_table[:].indirect(lists[i][:, a // 16 : b // 16]))
-                for column in range(a, b, QUARTER):
-                    where[i, column] = planes[n][:, at + column - a : at + column - a + QUARTER]
+                for left, right in STRETCHES:
+                    if a <= left < b:
+                        where[i, left] = planes[n][:, at + left - a : at + right - a]
                 at = at + b - a
             for s in range(4):
                 (nc.sync, nc.scalar)[s % 2].dma_start(planes[n][s:P:32, :].bitcast(I32), picked[8 * s : P : 32, :].bitcast(I32))
@@ -106,16 +107,14 @@ def tile_picked_phdiff_relu_p_kernel(tc, x_words, x_scales, w1, w2, offs, old, o
 
         early = keep.tile([M, HALF], F32, name="early")
         late = [keep.tile([M, QUARTER], F32, name="late%d" % c) for c in range(2)]
-        for c in range(2):
-            product(0, c, q1, now[:, c * QUARTER : (c + 1) * QUARTER])
-        for c in range(2):
-            product(1, c, q2, first[:, c * QUARTER : (c + 1) * QUARTER])
-            nc.scalar.activation(early[:, c * QUARTER : (c + 1) * QUARTER], acc[c][:], ACT.Relu)
+        product(0, 0, q1, now[:, :HALF])
+        product(1, 0, q2, first[:])
+        nc.scalar.activation(early[:], acc[0][:], ACT.Relu)
         nc.sync.dma_start(out[:, :HALF], early[:])
-        for c in range(2, 4):
-            product(0, c, q1, now[:, c * QUARTER : (c + 1) * QUARTER])
+        for c in range(1, 3):
+            product(0, c, q1, now[:, STRETCHES[c][0] : STRETCHES[c][1]])
         for c, queue in enumerate((nc.sync, nc.scalar)):
-            a, b = STRETCHES[2 + c]
-            product(1, 2 + c, q2, second[:, c * QUARTER : (c + 1) * QUARTER])
-            nc.scalar.activation(late[c][:], acc[2 + c][:], ACT.Relu)
+            a, b = STRETCHES[1 + c]
+            product(1, 1 + c, q2, second[:, c * QUARTER : (c + 1) * QUARTER])
+            nc.scalar.activation(late[c][:], acc[1 + c][:], ACT.Relu)
             queue.dma_start(out[:, a:b], late[c][:])

@@ -116,5 +116,8 @@ def tile_picked_phdiff_relu_p_kernel(tc, x_words, x_scales, w1, w2, offs, old, o
         for c, queue in enumerate((nc.sync, nc.scalar)):
             a, b = STRETCHES[1 + c]
             product(1, 1 + c, q2, second[:, c * QUARTER : (c + 1) * QUARTER])
-            nc.scalar.activation(late[c][:], acc[1 + c][:], ACT.Relu)
+            if c == 0:
+                nc.vector.tensor_scalar_max(late[c][:], acc[1 + c][:], 0.0)
+            else:
+                nc.scalar.activation(late[c][:], acc[1 + c][:], ACT.Relu)
             queue.dma_start(out[:, a:b], late[c][:])

@@ -113,10 +113,10 @@ def tile_picked_phdiff_relu_p_kernel(tc, x_words, x_scales, w1, w2, offs, old, o
         nc.sync.dma_start(out[:, :HALF], early[:])
         for c in range(1, 3):
             product(0, c, q1, now[:, STRETCHES[c][0] : STRETCHES[c][1]])
-        for c, queue in enumerate((nc.sync, nc.scalar)):
+        for c, queue in enumerate((nc.scalar, nc.sync)):
             a, b = STRETCHES[1 + c]
             product(1, 1 + c, q2, second[:, c * QUARTER : (c + 1) * QUARTER])
-            if c == 0:
+            if c == 1:
                 nc.vector.tensor_scalar_max(late[c][:], acc[1 + c][:], 0.0)
             else:
                 nc.scalar.activation(late[c][:], acc[1 + c][:], ACT.Relu)

@@ -18,7 +18,7 @@ P = 128
 PACK = 4
 HALF = S // 2
 QUARTER = S // 4
-STRETCHES = ((0, HALF), (HALF, HALF + QUARTER), (HALF + QUARTER, S))
+STRETCHES = tuple((c * QUARTER, (c + 1) * QUARTER) for c in range(4))
 EARLY = 128
 
 
@@ -107,17 +107,18 @@ def tile_picked_phdiff_relu_p_kernel(tc, x_words, x_scales, w1, w2, offs, old, o
 
         early = keep.tile([M, HALF], F32, name="early")
         late = [keep.tile([M, QUARTER], F32, name="late%d" % c) for c in range(2)]
-        product(0, 0, q1, now[:, :HALF])
-        product(1, 0, q2, first[:])
-        nc.scalar.activation(early[:], acc[0][:], ACT.Relu)
+        for c in range(2):
+            product(0, c, q1, now[:, c * QUARTER : (c + 1) * QUARTER])
+        for c in range(2):
+            product(1, c, q2, first[:, c * QUARTER : (c + 1) * QUARTER])
+        nc.scalar.activation(early[:, :QUARTER], acc[0][:], ACT.Relu)
+        nc.vector.tensor_scalar_max(early[:, QUARTER:], acc[1][:], 0.0)
         nc.sync.dma_start(out[:, :HALF], early[:])
-        for c in range(1, 3):
-            product(0, c, q1, now[:, STRETCHES[c][0] : STRETCHES[c][1]])
-        for c, queue in enumerate((nc.scalar, nc.sync)):
-            a, b = STRETCHES[1 + c]
-            product(1, 1 + c, q2, second[:, c * QUARTER : (c + 1) * QUARTER])
-            if c == 1:
-                nc.vector.tensor_scalar_max(late[c][:], acc[1 + c][:], 0.0)
-            else:
-                nc.scalar.activation(late[c][:], acc[1 + c][:], ACT.Relu)
-            queue.dma_start(out[:, a:b], late[c][:])
+        for c in range(2, 4):
+            product(0, c, q1, now[:, c * QUARTER : (c + 1) * QUARTER])
+        for c in range(2):
+            product(1, 2 + c, q2, second[:, c * QUARTER : (c + 1) * QUARTER])
+        nc.scalar.activation(late[0][:], acc[2][:], ACT.Relu)
+        nc.scalar.dma_start(out[:, HALF : HALF + QUARTER], late[0][:])
+        nc.vector.tensor_scalar_max(late[1][:], acc[3][:], 0.0)
+        nc.sync.dma_start(out[:, HALF + QUARTER :], late[1][:])

@@ -19,6 +19,7 @@ PACK = 4
 HALF = S // 2
 QUARTER = S // 4
 STRETCHES = tuple((c * QUARTER, (c + 1) * QUARTER) for c in range(4))
+ALIGN = 256
 EARLY = 128
 
 
@@ -28,26 +29,26 @@ def tile_picked_phdiff_relu_p_kernel(tc, x_words, x_scales, w1, w2, offs, old, o
         keep = ctx.enter_context(tc.tile_pool(name="keep", bufs=1))
         psum = ctx.enter_context(tc.psum_pool(name="psum", bufs=1))
 
-        scale_table = keep.tile([P, T], U8, name="scale_table", align_bytes=64)
+        scale_table = keep.tile([P, T], U8, name="scale_table", align_bytes=ALIGN)
         nc.vector.memset(scale_table[:].bitcast(I32), 0)
 
         lists = [keep.tile([P, S // 16], U16, name="list%d" % i) for i in range(2)]
         nc.sync.dma_start(lists[0][:], offs)
         nc.sync.dma_start(lists[1][:], old)
 
-        word_table = keep.tile([P, T], U32, name="word_table", align_bytes=64)
+        word_table = keep.tile([P, T], U32, name="word_table", align_bytes=ALIGN)
         words = x_words[0].rearrange("p n t -> p (n t)").bitcast(I32)
         for first_row in range(2):
             nc.scalar.dma_start(word_table[first_row:P:2, :EARLY].bitcast(I32), words[first_row:P:2, :EARLY])
         nc.scalar.dma_start(scale_table[0:P:8, :].bitcast(I32), x_scales[0].bitcast(I32))
         nc.scalar.dma_start(word_table[:, EARLY:].bitcast(I32), words[:, EARLY:])
-        raw = [keep.tile([P, PACK, M], F32, name="raw%d" % i, tag="slot%d" % i, align_bytes=64) for i in range(2)]
+        raw = [keep.tile([P, PACK, M], F32, name="raw%d" % i, tag="slot%d" % i, align_bytes=ALIGN) for i in range(2)]
         nc.scalar.dma_start(raw[0][:], w1.rearrange("(p j) m -> p j m", j=PACK))
         nc.scalar.dma_start(raw[1][:], w2.rearrange("(p j) m -> p j m", j=PACK))
 
         batches = (((0, 0, S), (1, 0, S)),)
         widths = [sum(b - a for i, a, b in batch) for batch in batches]
-        planes = [keep.tile([P, w], U8, name="plane%d" % n, align_bytes=64) for n, w in enumerate(widths)]
+        planes = [keep.tile([P, w], U8, name="plane%d" % n, align_bytes=ALIGN) for n, w in enumerate(widths)]
         for plane in planes:
             nc.vector.memset(plane[:].bitcast(I32), 0)
 
@@ -58,7 +59,7 @@ def tile_picked_phdiff_relu_p_kernel(tc, x_words, x_scales, w1, w2, offs, old, o
 
         where = {}
         for n, batch in enumerate(batches):
-            picked = keep.tile([P, widths[n]], U8, name="picked%d" % n, align_bytes=64)
+            picked = keep.tile([P, widths[n]], U8, name="picked%d" % n, align_bytes=ALIGN)
             at = 0
             for i, a, b in batch:
                 nc.vector.tensor_copy(picked[:, at : at + b - a], scale_table[:].indirect(lists[i][:, a // 16 : b // 16]))
@@ -70,15 +71,15 @@ def tile_picked_phdiff_relu_p_kernel(tc, x_words, x_scales, w1, w2, offs, old, o
                 (nc.sync, nc.scalar)[s % 2].dma_start(planes[n][s:P:32, :].bitcast(I32), picked[8 * s : P : 32, :].bitcast(I32))
 
         def quantize(i, sign):
-            grouped = keep.tile([P, M, PACK], BF16, name="grouped%d" % i, align_bytes=64)
+            grouped = keep.tile([P, M, PACK], BF16, name="grouped%d" % i, align_bytes=ALIGN)
             nc.scalar.activation(
                 grouped[:].rearrange("p (c i) j -> p c j i", i=PACK),
                 raw[i][:].rearrange("p j (c i) -> p c j i", i=PACK),
                 ACT.Copy,
                 scale=sign,
             )
-            w_codes = keep.tile([P, M], U32, name="w_codes%d" % i, align_bytes=64)
-            w_scales = keep.tile([P, M], U8, name="w_scales%d" % i, align_bytes=64)
+            w_codes = keep.tile([P, M], U32, name="w_codes%d" % i, align_bytes=ALIGN)
+            w_scales = keep.tile([P, M], U8, name="w_scales%d" % i, align_bytes=ALIGN)
             nc.vector.quantize_mx(out=w_codes[:].bitcast(FP8X4), scales=w_scales[:], in_=grouped[:].rearrange("p m j -> p (m j)"))
             return w_codes, w_scales
 
@@ -96,17 +97,17 @@ def tile_picked_phdiff_relu_p_kernel(tc, x_words, x_scales, w1, w2, offs, old, o
                 stop=(i == 1),
             )
 
-        now = keep.tile([P, S], U32, name="now", align_bytes=64)
+        now = keep.tile([P, S], U32, name="now", align_bytes=ALIGN)
         nc.vector.tensor_copy(now[:], word_table[:].indirect(lists[0][:]))
-        first = keep.tile([P, HALF], U32, name="first", align_bytes=64)
+        first = keep.tile([P, HALF], U32, name="first", align_bytes=ALIGN)
         nc.vector.tensor_copy(first[:], word_table[:].indirect(lists[1][:, : HALF // 16]))
         q1 = quantize(0, 1.0)
         q2 = quantize(1, minus[:])
-        second = keep.tile([P, HALF], U32, name="second", tag="slot1", align_bytes=64)
+        second = keep.tile([P, HALF], U32, name="second", tag="slot1", align_bytes=ALIGN)
         nc.vector.tensor_copy(second[:], word_table[:].indirect(lists[1][:, HALF // 16 :]))
 
-        early = keep.tile([M, HALF], F32, name="early")
-        late = [keep.tile([M, QUARTER], F32, name="late%d" % c) for c in range(2)]
+        early = keep.tile([M, HALF], F32, name="early", align_bytes=ALIGN)
+        late = [keep.tile([M, QUARTER], F32, name="late%d" % c, align_bytes=ALIGN) for c in range(2)]
         for c in range(2):
             product(0, c, q1, now[:, c * QUARTER : (c + 1) * QUARTER])
         for c in range(2):

from contextlib import ExitStack

import concourse.mybir as mybir

K, T, S, M = 512, 2048, 512, 128
FLOPS = 2 * 2 * K * M * S

F32 = mybir.dt.float32
BF16 = mybir.dt.bfloat16
I32 = mybir.dt.int32
U32 = mybir.dt.uint32
U16 = mybir.dt.uint16
U8 = mybir.dt.uint8
FP8X4 = mybir.dt.float8_e4m3fn_x4
ACT = mybir.ActivationFunctionType

P = 128
PACK = 4
HALF = S // 2
QUARTER = S // 4
STRETCHES = tuple((c * QUARTER, (c + 1) * QUARTER) for c in range(4))
ALIGN = 256
EARLY = 128


def tile_picked_phdiff_relu_p_kernel(tc, x_words, x_scales, w1, w2, offs, old, out):
    nc = tc.nc
    with ExitStack() as ctx:
        keep = ctx.enter_context(tc.tile_pool(name="keep", bufs=1))
        psum = ctx.enter_context(tc.psum_pool(name="psum", bufs=1))

        scale_table = keep.tile([P, T], U8, name="scale_table", align_bytes=ALIGN)
        nc.vector.memset(scale_table[:].bitcast(I32), 0)

        lists = [keep.tile([P, S // 16], U16, name="list%d" % i) for i in range(2)]
        nc.sync.dma_start(lists[0][:], offs)
        nc.sync.dma_start(lists[1][:], old)

        word_table = keep.tile([P, T], U32, name="word_table", align_bytes=ALIGN)
        words = x_words[0].rearrange("p n t -> p (n t)").bitcast(I32)
        for first_row in range(2):
            nc.scalar.dma_start(word_table[first_row:P:2, :EARLY].bitcast(I32), words[first_row:P:2, :EARLY])
        nc.scalar.dma_start(scale_table[0:P:8, :].bitcast(I32), x_scales[0].bitcast(I32))
        nc.scalar.dma_start(word_table[:, EARLY:].bitcast(I32), words[:, EARLY:])
        raw = [keep.tile([P, PACK, M], F32, name="raw%d" % i, tag="slot%d" % i, align_bytes=ALIGN) for i in range(2)]
        nc.scalar.dma_start(raw[0][:], w1.rearrange("(p j) m -> p j m", j=PACK))
        nc.scalar.dma_start(raw[1][:], w2.rearrange("(p j) m -> p j m", j=PACK))

        batches = (((0, 0, S), (1, 0, S)),)
        widths = [sum(b - a for i, a, b in batch) for batch in batches]
        planes = [keep.tile([P, w], U8, name="plane%d" % n, align_bytes=ALIGN) for n, w in enumerate(widths)]
        for plane in planes:
            nc.vector.memset(plane[:].bitcast(I32), 0)

        one = keep.tile([P, 1], F32, name="one")
        nc.vector.memset(one[:], 1.0)
        minus = keep.tile([P, 1], F32, name="minus")
        nc.scalar.activation(minus[:], one[:], ACT.Copy, scale=-1.0)

        where = {}
        for n, batch in enumerate(batches):
            picked = keep.tile([P, widths[n]], U8, name="picked%d" % n, align_bytes=ALIGN)
            at = 0
            for i, a, b in batch:
                nc.vector.tensor_copy(picked[:, at : at + b - a], scale_table[:].indirect(lists[i][:, a // 16 : b // 16]))
                for left, right in STRETCHES:
                    if a <= left < b:
                        where[i, left] = planes[n][:, at + left - a : at + right - a]
                at = at + b - a
            for s in range(4):
                (nc.sync, nc.scalar)[s % 2].dma_start(planes[n][s:P:32, :].bitcast(I32), picked[8 * s : P : 32, :].bitcast(I32))

        def quantize(i, sign):
            grouped = keep.tile([P, M, PACK], BF16, name="grouped%d" % i, align_bytes=ALIGN)
            nc.scalar.activation(
                grouped[:].rearrange("p (c i) j -> p c j i", i=PACK),
                raw[i][:].rearrange("p j (c i) -> p c j i", i=PACK),
                ACT.Copy,
                scale=sign,
            )
            w_codes = keep.tile([P, M], U32, name="w_codes%d" % i, align_bytes=ALIGN)
            w_scales = keep.tile([P, M], U8, name="w_scales%d" % i, align_bytes=ALIGN)
            nc.vector.quantize_mx(out=w_codes[:].bitcast(FP8X4), scales=w_scales[:], in_=grouped[:].rearrange("p m j -> p (m j)"))
            return w_codes, w_scales

        acc = [psum.tile([M, b - a], F32, name="acc%d" % a) for a, b in STRETCHES]

        def product(i, c, weights, moving):
            a, b = STRETCHES[c]
            nc.tensor.matmul_mx(
                out=acc[c][:],
                lhsT=weights[0][:].bitcast(FP8X4),
                lhsT_scale=weights[1][:],
                rhs=moving.bitcast(FP8X4),
                rhs_scale=where[i, a],
                start=(i == 0),
                stop=(i == 1),
            )

        now = keep.tile([P, S], U32, name="now", align_bytes=ALIGN)
        nc.vector.tensor_copy(now[:], word_table[:].indirect(lists[0][:]))
        first = keep.tile([P, HALF], U32, name="first", align_bytes=ALIGN)
        nc.vector.tensor_copy(first[:], word_table[:].indirect(lists[1][:, : HALF // 16]))
        q1 = quantize(0, 1.0)
        q2 = quantize(1, minus[:])
        second = keep.tile([P, HALF], U32, name="second", tag="slot1", align_bytes=ALIGN)
        nc.vector.tensor_copy(second[:], word_table[:].indirect(lists[1][:, HALF // 16 :]))

        early = keep.tile([M, HALF], F32, name="early", align_bytes=ALIGN)
        late = [keep.tile([M, QUARTER], F32, name="late%d" % c, align_bytes=ALIGN) for c in range(2)]
        for c in range(2):
            product(0, c, q1, now[:, c * QUARTER : (c + 1) * QUARTER])
        for c in range(2):
            product(1, c, q2, first[:, c * QUARTER : (c + 1) * QUARTER])
        nc.scalar.activation(early[:, :QUARTER], acc[0][:], ACT.Relu)
        nc.vector.tensor_scalar_max(early[:, QUARTER:], acc[1][:], 0.0)
        nc.sync.dma_start(out[:, :HALF], early[:])
        for c in range(2, 4):
            product(0, c, q1, now[:, c * QUARTER : (c + 1) * QUARTER])
        for c in range(2):
            product(1, 2 + c, q2, second[:, c * QUARTER : (c + 1) * QUARTER])
        nc.scalar.activation(late[0][:], acc[2][:], ACT.Relu)
        nc.scalar.dma_start(out[:, HALF : HALF + QUARTER], late[0][:])
        nc.vector.tensor_scalar_max(late[1][:], acc[3][:], 0.0)
        nc.sync.dma_start(out[:, HALF + QUARTER :], late[1][:])
